import numpy as np
import ml_dtypes

BF16 = ml_dtypes.bfloat16


def bf(x):
    return np.asarray(x, np.float32).astype(BF16)


def f32(x):
    return np.asarray(x, np.float32)


def f64(x):
    return np.asarray(x).astype(np.float64)


def striped(idx):
    return np.tile(idx.reshape(-1, 16).T, (8, 1))


def rows(idx, k):
    return np.tile(idx, (k, 1))


def look(tab, idx):
    return np.take_along_axis(f64(tab), rows(idx, len(tab)), axis=1)


K, S, V, N = 256, 2048, 512, 512


def silu(v):
    return v / (1.0 + np.exp(-v))


def setup_inputs():
    return {"tab": f32(np.random.standard_normal((2, K, S))), "y": f32(np.random.standard_normal((K, V))), "offs": striped(np.random.permutation(S)[:N])}


def reference(tab, y, offs):
    idx = offs[:16].T.reshape(-1)
    x = (look(tab[0], idx) + f64(y)) * (silu(look(tab[1], idx)))
    return x

@@ -1,0 +1,46 @@
+import concourse.mybir as mybir
+
+F32 = mybir.dt.float32
+U16 = mybir.dt.uint16
+ADD = mybir.AluOpType.add
+MULT = mybir.AluOpType.mult
+SILU = mybir.ActivationFunctionType.Silu
+
+P = 128
+PIECES = 2
+
+
+def tile_lookup_vg_addsilu_out_kernel(tc, tab, y, offs, out):
+    nc = tc.nc
+    rows, places = tab.shape[1], tab.shape[2]
+    n = y.shape[1]
+    blocks = rows // P
+
+    with tc.tile_pool(name="held", bufs=1) as held:
+        offsets = held.tile([P, n // 16], U16, name="offsets")
+        streams = held.tile([P, blocks, n], F32, name="streams")
+
+        gates, values = [], []
+        for b in range(blocks):
+            block = slice(b * P, (b + 1) * P)
+            gate = held.tile([P, places], F32, name=f"gate{b}")
+            nc.sync.dma_start(gate[:], tab[1, block, :])
+            if b == 0:
+                nc.sync.dma_start(offsets[:], offs)
+                nc.sync.dma_start(streams[:], y.rearrange("(b p) n -> p b n", p=P))
+            value = held.tile([P, places], F32, name=f"value{b}")
+            nc.sync.dma_start(value[:], tab[0, block, :])
+            gates.append(gate)
+            values.append(value)
+
+        for b in range(blocks):
+            opened = held.tile([P, n], F32, name=f"opened{b}")
+            nc.scalar.activation(opened[:], gates[b][:].indirect(offsets[:]), SILU)
+            for h in range(PIECES):
+                part = slice(h * n // PIECES, (h + 1) * n // PIECES)
+                part_offsets = offsets[:, h * n // 16 // PIECES : (h + 1) * n // 16 // PIECES]
+                summed = held.tile([P, n // PIECES], F32, name=f"summed{b}_{h}")
+                nc.vector.tensor_tensor(summed[:], values[b][:].indirect(part_offsets), streams[:, b, part], ADD)
+                product = held.tile([P, n // PIECES], F32, name=f"product{b}_{h}")
+                nc.vector.tensor_tensor(product[:], summed[:], opened[:, part], MULT)
+                nc.sync.dma_start(out[b * P : (b + 1) * P, part], product[:])

@@ -7,40 +7,54 @@ MULT = mybir.AluOpType.mult
 SILU = mybir.ActivationFunctionType.Silu
 
 P = 128
-PIECES = 2
+SUM_CUTS = (0, 192, 352, 512)
+PRODUCT_CUTS = (0, 256, 384, 512)
 
 
 def tile_lookup_vg_addsilu_out_kernel(tc, tab, y, offs, out):
     nc = tc.nc
-    rows, places = tab.shape[1], tab.shape[2]
+    places = tab.shape[2]
     n = y.shape[1]
-    blocks = rows // P
+    tab_rows = tab.rearrange("t (p b) s -> t b p s", b=2)
+    y_rows = y.rearrange("(p b) n -> p (b n)", b=2)
+    out_rows = out.rearrange("(p b) n -> b p n", b=2)
+    early = n + SUM_CUTS[1]
 
     with tc.tile_pool(name="held", bufs=1) as held:
         offsets = held.tile([P, n // 16], U16, name="offsets")
-        streams = held.tile([P, blocks, n], F32, name="streams")
+        gates = [held.tile([P, places], F32, name=f"gate{b}") for b in range(2)]
+        values = [held.tile([P, places], F32, name=f"value{b}") for b in range(2)]
+        y_early = held.tile([P, early], F32, name="y_early")
+        y_late = held.tile([P, 2 * n - early], F32, name="y_late")
 
-        gates, values = [], []
-        for b in range(blocks):
-            block = slice(b * P, (b + 1) * P)
-            gate = held.tile([P, places], F32, name=f"gate{b}")
-            nc.sync.dma_start(gate[:], tab[1, block, :])
-            if b == 0:
-                nc.sync.dma_start(offsets[:], offs)
-                nc.sync.dma_start(streams[:], y.rearrange("(b p) n -> p b n", p=P))
-            value = held.tile([P, places], F32, name=f"value{b}")
-            nc.sync.dma_start(value[:], tab[0, block, :])
-            gates.append(gate)
-            values.append(value)
+        nc.sync.dma_start(gates[0][:], tab_rows[1, 0])
+        nc.sync.dma_start(offsets[:], offs)
+        nc.sync.dma_start(y_early[:], y_rows[:, :early])
+        nc.sync.dma_start(values[0][:], tab_rows[0, 0])
+        nc.sync.dma_start(gates[1][:], tab_rows[1, 1])
+        nc.sync.dma_start(values[1][:], tab_rows[0, 1])
+        nc.sync.dma_start(y_late[:], y_rows[:, early:])
 
-        for b in range(blocks):
-            opened = held.tile([P, n], F32, name=f"opened{b}")
-            nc.scalar.activation(opened[:], gates[b][:].indirect(offsets[:]), SILU)
-            for h in range(PIECES):
-                part = slice(h * n // PIECES, (h + 1) * n // PIECES)
-                part_offsets = offsets[:, h * n // 16 // PIECES : (h + 1) * n // 16 // PIECES]
-                summed = held.tile([P, n // PIECES], F32, name=f"summed{b}_{h}")
-                nc.vector.tensor_tensor(summed[:], values[b][:].indirect(part_offsets), streams[:, b, part], ADD)
-                product = held.tile([P, n // PIECES], F32, name=f"product{b}_{h}")
-                nc.vector.tensor_tensor(product[:], summed[:], opened[:, part], MULT)
-                nc.sync.dma_start(out[b * P : (b + 1) * P, part], product[:])
+        opened = [held.tile([P, n], F32, name=f"opened{b}") for b in range(2)]
+        summed = [held.tile([P, n], F32, name=f"summed{b}") for b in range(2)]
+        product = [held.tile([P, n], F32, name=f"product{b}") for b in range(2)]
+        for b in range(2):
+            nc.scalar.activation(opened[b][:], gates[b][:].indirect(offsets[:]), SILU)
+
+        def add(b, lo, hi, stream):
+            picked = values[b][:].indirect(offsets[:, lo // 16 : hi // 16])
+            nc.vector.tensor_tensor(summed[b][:, lo:hi], picked, stream, ADD)
+
+        def multiply_and_store(b, lo, hi):
+            nc.vector.tensor_tensor(product[b][:, lo:hi], summed[b][:, lo:hi], opened[b][:, lo:hi], MULT)
+            nc.sync.dma_start(out_rows[b, :, lo:hi], product[b][:, lo:hi])
+
+        add(0, 0, n, y_early[:, :n])
+        multiply_and_store(0, 0, n)
+
+        first, second, third, end = SUM_CUTS
+        add(1, first, second, y_early[:, n:])
+        add(1, second, third, y_late[:, : third - second])
+        add(1, third, end, y_late[:, third - second :])
+        for lo, hi in zip(PRODUCT_CUTS, PRODUCT_CUTS[1:]):
+            multiply_and_store(1, lo, hi)

@@ -7,8 +7,14 @@ MULT = mybir.AluOpType.mult
 SILU = mybir.ActivationFunctionType.Silu
 
 P = 128
+Y_CUTS = (192, 512)
 SUM_CUTS = (0, 192, 352, 512)
 PRODUCT_CUTS = (0, 256, 384, 512)
+STORE_CUTS = (0, 96, 192, 288, 384, 448, 512)
+
+
+def pieces(cuts):
+    return list(zip(cuts, cuts[1:]))
 
 
 def tile_lookup_vg_addsilu_out_kernel(tc, tab, y, offs, out):
@@ -18,22 +24,21 @@ def tile_lookup_vg_addsilu_out_kernel(tc, tab, y, offs, out):
     tab_rows = tab.rearrange("t (p b) s -> t b p s", b=2)
     y_rows = y.rearrange("(p b) n -> p (b n)", b=2)
     out_rows = out.rearrange("(p b) n -> b p n", b=2)
-    early = n + SUM_CUTS[1]
 
     with tc.tile_pool(name="held", bufs=1) as held:
         offsets = held.tile([P, n // 16], U16, name="offsets")
         gates = [held.tile([P, places], F32, name=f"gate{b}") for b in range(2)]
         values = [held.tile([P, places], F32, name=f"value{b}") for b in range(2)]
-        y_early = held.tile([P, early], F32, name="y_early")
-        y_late = held.tile([P, 2 * n - early], F32, name="y_late")
+        stream = held.tile([P, 2 * n], F32, name="stream")
 
         nc.sync.dma_start(gates[0][:], tab_rows[1, 0])
         nc.sync.dma_start(offsets[:], offs)
-        nc.sync.dma_start(y_early[:], y_rows[:, :early])
+        nc.sync.dma_start(stream[:, : n + Y_CUTS[0]], y_rows[:, : n + Y_CUTS[0]])
         nc.sync.dma_start(values[0][:], tab_rows[0, 0])
         nc.sync.dma_start(gates[1][:], tab_rows[1, 1])
         nc.sync.dma_start(values[1][:], tab_rows[0, 1])
-        nc.sync.dma_start(y_late[:], y_rows[:, early:])
+        for lo, hi in pieces(Y_CUTS):
+            nc.sync.dma_start(stream[:, n + lo : n + hi], y_rows[:, n + lo : n + hi])
 
         opened = [held.tile([P, n], F32, name=f"opened{b}") for b in range(2)]
         summed = [held.tile([P, n], F32, name=f"summed{b}") for b in range(2)]
@@ -41,20 +46,23 @@ def tile_lookup_vg_addsilu_out_kernel(tc, tab, y, offs, out):
         for b in range(2):
             nc.scalar.activation(opened[b][:], gates[b][:].indirect(offsets[:]), SILU)
 
-        def add(b, lo, hi, stream):
+        def add(b, lo, hi):
             picked = values[b][:].indirect(offsets[:, lo // 16 : hi // 16])
-            nc.vector.tensor_tensor(summed[b][:, lo:hi], picked, stream, ADD)
+            nc.vector.tensor_tensor(summed[b][:, lo:hi], picked, stream[:, b * n + lo : b * n + hi], ADD)
 
-        def multiply_and_store(b, lo, hi):
+        def multiply(b, lo, hi):
             nc.vector.tensor_tensor(product[b][:, lo:hi], summed[b][:, lo:hi], opened[b][:, lo:hi], MULT)
+
+        def store(b, lo, hi):
             nc.sync.dma_start(out_rows[b, :, lo:hi], product[b][:, lo:hi])
 
-        add(0, 0, n, y_early[:, :n])
-        multiply_and_store(0, 0, n)
+        add(0, 0, n)
+        multiply(0, 0, n)
+        for lo, hi in pieces(STORE_CUTS):
+            store(0, lo, hi)
 
-        first, second, third, end = SUM_CUTS
-        add(1, first, second, y_early[:, n:])
-        add(1, second, third, y_late[:, : third - second])
-        add(1, third, end, y_late[:, third - second :])
-        for lo, hi in zip(PRODUCT_CUTS, PRODUCT_CUTS[1:]):
-            multiply_and_store(1, lo, hi)
+        for lo, hi in pieces(SUM_CUTS):
+            add(1, lo, hi)
+        for lo, hi in pieces(PRODUCT_CUTS):
+            multiply(1, lo, hi)
+            store(1, lo, hi)

@@ -7,10 +7,10 @@ MULT = mybir.AluOpType.mult
 SILU = mybir.ActivationFunctionType.Silu
 
 P = 128
-Y_CUTS = (192, 512)
+DMA_BLOCK = 256
 SUM_CUTS = (0, 192, 352, 512)
-PRODUCT_CUTS = (0, 256, 384, 512)
-STORE_CUTS = (0, 96, 192, 288, 384, 448, 512)
+PRODUCT_CUTS = (0, 128, 320, 512)
+STORE_CUTS = (0, 128, 192, 256, 320, 384, 512)
 
 
 def pieces(cuts):
@@ -24,25 +24,29 @@ def tile_lookup_vg_addsilu_out_kernel(tc, tab, y, offs, out):
     tab_rows = tab.rearrange("t (p b) s -> t b p s", b=2)
     y_rows = y.rearrange("(p b) n -> p (b n)", b=2)
     out_rows = out.rearrange("(p b) n -> b p n", b=2)
+    early = n + SUM_CUTS[1]
 
     with tc.tile_pool(name="held", bufs=1) as held:
+
+        def float_tile(name, columns):
+            return held.tile([P, columns], F32, name=name, align_bytes=DMA_BLOCK)
+
         offsets = held.tile([P, n // 16], U16, name="offsets")
-        gates = [held.tile([P, places], F32, name=f"gate{b}") for b in range(2)]
-        values = [held.tile([P, places], F32, name=f"value{b}") for b in range(2)]
-        stream = held.tile([P, 2 * n], F32, name="stream")
+        gates = [float_tile(f"gate{b}", places) for b in range(2)]
+        values = [float_tile(f"value{b}", places) for b in range(2)]
+        stream = float_tile("stream", 2 * n)
 
         nc.sync.dma_start(gates[0][:], tab_rows[1, 0])
         nc.sync.dma_start(offsets[:], offs)
-        nc.sync.dma_start(stream[:, : n + Y_CUTS[0]], y_rows[:, : n + Y_CUTS[0]])
+        nc.sync.dma_start(stream[:, :early], y_rows[:, :early])
         nc.sync.dma_start(values[0][:], tab_rows[0, 0])
         nc.sync.dma_start(gates[1][:], tab_rows[1, 1])
         nc.sync.dma_start(values[1][:], tab_rows[0, 1])
-        for lo, hi in pieces(Y_CUTS):
-            nc.sync.dma_start(stream[:, n + lo : n + hi], y_rows[:, n + lo : n + hi])
+        nc.sync.dma_start(stream[:, early:], y_rows[:, early:])
 
-        opened = [held.tile([P, n], F32, name=f"opened{b}") for b in range(2)]
-        summed = [held.tile([P, n], F32, name=f"summed{b}") for b in range(2)]
-        product = [held.tile([P, n], F32, name=f"product{b}") for b in range(2)]
+        opened = [float_tile(f"opened{b}", n) for b in range(2)]
+        summed = [float_tile(f"summed{b}", n) for b in range(2)]
+        product = [float_tile(f"product{b}", n) for b in range(2)]
         for b in range(2):
             nc.scalar.activation(opened[b][:], gates[b][:].indirect(offsets[:]), SILU)
 
@@ -50,19 +54,17 @@ def tile_lookup_vg_addsilu_out_kernel(tc, tab, y, offs, out):
             picked = values[b][:].indirect(offsets[:, lo // 16 : hi // 16])
             nc.vector.tensor_tensor(summed[b][:, lo:hi], picked, stream[:, b * n + lo : b * n + hi], ADD)
 
-        def multiply(b, lo, hi):
-            nc.vector.tensor_tensor(product[b][:, lo:hi], summed[b][:, lo:hi], opened[b][:, lo:hi], MULT)
-
-        def store(b, lo, hi):
-            nc.sync.dma_start(out_rows[b, :, lo:hi], product[b][:, lo:hi])
+        def multiply(b, lo, hi, into):
+            nc.vector.tensor_tensor(into, summed[b][:, lo:hi], opened[b][:, lo:hi], MULT)
 
         add(0, 0, n)
-        multiply(0, 0, n)
+        multiply(0, 0, n, product[0][:])
         for lo, hi in pieces(STORE_CUTS):
-            store(0, lo, hi)
+            nc.sync.dma_start(out_rows[0, :, lo:hi], product[0][:, lo:hi])
 
         for lo, hi in pieces(SUM_CUTS):
             add(1, lo, hi)
         for lo, hi in pieces(PRODUCT_CUTS):
-            multiply(1, lo, hi)
-            store(1, lo, hi)
+            into = stream[:, early : early + hi] if lo == 0 else product[1][:, lo:hi]
+            multiply(1, lo, hi, into)
+            nc.sync.dma_start(out_rows[1, :, lo:hi], into)

@@ -8,9 +8,10 @@ SILU = mybir.ActivationFunctionType.Silu
 
 P = 128
 DMA_BLOCK = 256
-SUM_CUTS = (0, 192, 352, 512)
+Y_CUTS = (64, 192, 512)
+SUM_CUTS = (0, 64, 192, 352, 512)
 PRODUCT_CUTS = (0, 128, 320, 512)
-STORE_CUTS = (0, 128, 192, 256, 320, 384, 512)
+STORE_CUTS = (0, 128, 256, 320, 384, 512)
 
 
 def pieces(cuts):
@@ -24,7 +25,7 @@ def tile_lookup_vg_addsilu_out_kernel(tc, tab, y, offs, out):
     tab_rows = tab.rearrange("t (p b) s -> t b p s", b=2)
     y_rows = y.rearrange("(p b) n -> p (b n)", b=2)
     out_rows = out.rearrange("(p b) n -> b p n", b=2)
-    early = n + SUM_CUTS[1]
+    early, last = n + Y_CUTS[0], n + Y_CUTS[1]
 
     with tc.tile_pool(name="held", bufs=1) as held:
 
@@ -42,7 +43,8 @@ def tile_lookup_vg_addsilu_out_kernel(tc, tab, y, offs, out):
         nc.sync.dma_start(values[0][:], tab_rows[0, 0])
         nc.sync.dma_start(gates[1][:], tab_rows[1, 1])
         nc.sync.dma_start(values[1][:], tab_rows[0, 1])
-        nc.sync.dma_start(stream[:, early:], y_rows[:, early:])
+        nc.sync.dma_start(stream[:, early:last], y_rows[:, early:last])
+        nc.sync.dma_start(stream[:, last:], y_rows[:, last:])
 
         opened = [float_tile(f"opened{b}", n) for b in range(2)]
         summed = [float_tile(f"summed{b}", n) for b in range(2)]
@@ -65,6 +67,6 @@ def tile_lookup_vg_addsilu_out_kernel(tc, tab, y, offs, out):
         for lo, hi in pieces(SUM_CUTS):
             add(1, lo, hi)
         for lo, hi in pieces(PRODUCT_CUTS):
-            into = stream[:, early : early + hi] if lo == 0 else product[1][:, lo:hi]
+            into = stream[:, last : last + hi] if lo == 0 else product[1][:, lo:hi]
             multiply(1, lo, hi, into)
             nc.sync.dma_start(out_rows[1, :, lo:hi], into)

@@ -11,7 +11,7 @@ DMA_BLOCK = 256
 Y_CUTS = (64, 192, 512)
 SUM_CUTS = (0, 64, 192, 352, 512)
 PRODUCT_CUTS = (0, 128, 320, 512)
-STORE_CUTS = (0, 128, 256, 320, 384, 512)
+STORE_CUTS = (0, 128, 256, 320, 384, 448, 512)
 
 
 def pieces(cuts):
@@ -22,7 +22,8 @@ def tile_lookup_vg_addsilu_out_kernel(tc, tab, y, offs, out):
     nc = tc.nc
     places = tab.shape[2]
     n = y.shape[1]
-    tab_rows = tab.rearrange("t (p b) s -> t b p s", b=2)
+    gate_rows = tab[1].rearrange("(p b) s -> p (b s)", b=2)
+    value_rows = tab[0].rearrange("(p b) s -> b p s", b=2)
     y_rows = y.rearrange("(p b) n -> p (b n)", b=2)
     out_rows = out.rearrange("(p b) n -> b p n", b=2)
     early, last = n + Y_CUTS[0], n + Y_CUTS[1]
@@ -33,23 +34,24 @@ def tile_lookup_vg_addsilu_out_kernel(tc, tab, y, offs, out):
             return held.tile([P, columns], F32, name=name, align_bytes=DMA_BLOCK)
 
         offsets = held.tile([P, n // 16], U16, name="offsets")
-        gates = [float_tile(f"gate{b}", places) for b in range(2)]
+        both_gates = float_tile("both_gates", 2 * places)
         values = [float_tile(f"value{b}", places) for b in range(2)]
         stream = float_tile("stream", 2 * n)
 
-        nc.sync.dma_start(gates[0][:], tab_rows[1, 0])
+        nc.sync.dma_start(both_gates[:], gate_rows)
         nc.sync.dma_start(offsets[:], offs)
         nc.sync.dma_start(stream[:, :early], y_rows[:, :early])
-        nc.sync.dma_start(values[0][:], tab_rows[0, 0])
-        nc.sync.dma_start(gates[1][:], tab_rows[1, 1])
-        nc.sync.dma_start(values[1][:], tab_rows[0, 1])
+        nc.sync.dma_start(values[0][:], value_rows[0])
+        nc.sync.dma_start(values[1][:], value_rows[1])
         nc.sync.dma_start(stream[:, early:last], y_rows[:, early:last])
         nc.sync.dma_start(stream[:, last:], y_rows[:, last:])
 
+        gates = [float_tile(f"gate{b}", places) for b in range(2)]
         opened = [float_tile(f"opened{b}", n) for b in range(2)]
         summed = [float_tile(f"summed{b}", n) for b in range(2)]
         product = [float_tile(f"product{b}", n) for b in range(2)]
         for b in range(2):
+            nc.vector.tensor_copy(gates[b][:], both_gates[:, b * places : (b + 1) * places])
             nc.scalar.activation(opened[b][:], gates[b][:].indirect(offsets[:]), SILU)
 
         def add(b, lo, hi):
@@ -59,8 +61,11 @@ def tile_lookup_vg_addsilu_out_kernel(tc, tab, y, offs, out):
         def multiply(b, lo, hi, into):
             nc.vector.tensor_tensor(into, summed[b][:, lo:hi], opened[b][:, lo:hi], MULT)
 
-        add(0, 0, n)
-        multiply(0, 0, n, product[0][:])
+        halves = pieces((0, n // 2, n))
+        for lo, hi in halves:
+            add(0, lo, hi)
+        for lo, hi in halves:
+            multiply(0, lo, hi, product[0][:, lo:hi])
         for lo, hi in pieces(STORE_CUTS):
             nc.sync.dma_start(out_rows[0, :, lo:hi], product[0][:, lo:hi])
 

@@ -10,8 +10,8 @@ P = 128
 DMA_BLOCK = 256
 Y_CUTS = (64, 192, 512)
 SUM_CUTS = (0, 64, 192, 352, 512)
-PRODUCT_CUTS = (0, 128, 320, 512)
-STORE_CUTS = (0, 128, 256, 320, 384, 448, 512)
+PRODUCT_CUTS = (0, 128, 256, 384, 512)
+STORE_CUTS = (0, 128, 256, 384, 448, 512)
 
 
 def pieces(cuts):
@@ -71,7 +71,7 @@ def tile_lookup_vg_addsilu_out_kernel(tc, tab, y, offs, out):
 
         for lo, hi in pieces(SUM_CUTS):
             add(1, lo, hi)
-        for lo, hi in pieces(PRODUCT_CUTS):
+        for k, (lo, hi) in enumerate(pieces(PRODUCT_CUTS)):
             into = stream[:, last : last + hi] if lo == 0 else product[1][:, lo:hi]
             multiply(1, lo, hi, into)
-            nc.sync.dma_start(out_rows[1, :, lo:hi], into)
+            (nc.sync if k % 2 else nc.scalar).dma_start(out_rows[1, :, lo:hi], into)

@@ -10,8 +10,7 @@ P = 128
 DMA_BLOCK = 256
 Y_CUTS = (64, 192, 512)
 SUM_CUTS = (0, 64, 192, 352, 512)
-PRODUCT_CUTS = (0, 128, 256, 384, 512)
-STORE_CUTS = (0, 128, 256, 384, 448, 512)
+STORE_CUTS = (0, 128, 256, 384, 512)
 
 
 def pieces(cuts):
@@ -22,11 +21,10 @@ def tile_lookup_vg_addsilu_out_kernel(tc, tab, y, offs, out):
     nc = tc.nc
     places = tab.shape[2]
     n = y.shape[1]
-    gate_rows = tab[1].rearrange("(p b) s -> p (b s)", b=2)
     value_rows = tab[0].rearrange("(p b) s -> b p s", b=2)
+    gate_rows = tab[1].rearrange("(p b) s -> b p s", b=2)
     y_rows = y.rearrange("(p b) n -> p (b n)", b=2)
     out_rows = out.rearrange("(p b) n -> b p n", b=2)
-    early, last = n + Y_CUTS[0], n + Y_CUTS[1]
 
     with tc.tile_pool(name="held", bufs=1) as held:
 
@@ -34,25 +32,24 @@ def tile_lookup_vg_addsilu_out_kernel(tc, tab, y, offs, out):
             return held.tile([P, columns], F32, name=name, align_bytes=DMA_BLOCK)
 
         offsets = held.tile([P, n // 16], U16, name="offsets")
-        both_gates = float_tile("both_gates", 2 * places)
+        gates = [float_tile(f"gate{b}", places) for b in range(2)]
         values = [float_tile(f"value{b}", places) for b in range(2)]
         stream = float_tile("stream", 2 * n)
 
-        nc.sync.dma_start(both_gates[:], gate_rows)
+        nc.sync.dma_start(gates[0][:], gate_rows[0])
         nc.sync.dma_start(offsets[:], offs)
-        nc.sync.dma_start(stream[:, :early], y_rows[:, :early])
-        nc.sync.dma_start(values[0][:], value_rows[0])
+        nc.sync.dma_start(gates[1][:], gate_rows[1])
+        nc.scalar.dma_start(stream[:, : n + Y_CUTS[0]], y_rows[:, : n + Y_CUTS[0]])
+        nc.scalar.dma_start(values[0][:], value_rows[0])
         nc.sync.dma_start(values[1][:], value_rows[1])
-        nc.sync.dma_start(stream[:, early:last], y_rows[:, early:last])
-        nc.sync.dma_start(stream[:, last:], y_rows[:, last:])
+        for lo, hi in pieces(Y_CUTS):
+            nc.sync.dma_start(stream[:, n + lo : n + hi], y_rows[:, n + lo : n + hi])
 
-        gates = [float_tile(f"gate{b}", places) for b in range(2)]
         opened = [float_tile(f"opened{b}", n) for b in range(2)]
+        for b in range(2):
+            nc.scalar.activation(opened[b][:], gates[b][:].indirect(offsets[:]), SILU)
         summed = [float_tile(f"summed{b}", n) for b in range(2)]
         product = [float_tile(f"product{b}", n) for b in range(2)]
-        for b in range(2):
-            nc.vector.tensor_copy(gates[b][:], both_gates[:, b * places : (b + 1) * places])
-            nc.scalar.activation(opened[b][:], gates[b][:].indirect(offsets[:]), SILU)
 
         def add(b, lo, hi):
             picked = values[b][:].indirect(offsets[:, lo // 16 : hi // 16])
@@ -71,7 +68,7 @@ def tile_lookup_vg_addsilu_out_kernel(tc, tab, y, offs, out):
 
         for lo, hi in pieces(SUM_CUTS):
             add(1, lo, hi)
-        for k, (lo, hi) in enumerate(pieces(PRODUCT_CUTS)):
-            into = stream[:, last : last + hi] if lo == 0 else product[1][:, lo:hi]
+        for k, (lo, hi) in enumerate(pieces(STORE_CUTS)):
+            into = stream[:, n + SUM_CUTS[2] : n + SUM_CUTS[2] + hi] if k == 0 else product[1][:, lo:hi]
             multiply(1, lo, hi, into)
             (nc.sync if k % 2 else nc.scalar).dma_start(out_rows[1, :, lo:hi], into)

@@ -8,8 +8,8 @@ SILU = mybir.ActivationFunctionType.Silu
 
 P = 128
 DMA_BLOCK = 256
-Y_CUTS = (64, 192, 512)
-SUM_CUTS = (0, 64, 192, 352, 512)
+Y_CUTS = (0, 128, 448)
+SUMS = ((448, 512), (0, 128), (128, 256), (256, 448))
 STORE_CUTS = (0, 128, 256, 384, 512)
 
 
@@ -21,10 +21,13 @@ def tile_lookup_vg_addsilu_out_kernel(tc, tab, y, offs, out):
     nc = tc.nc
     places = tab.shape[2]
     n = y.shape[1]
-    value_rows = tab[0].rearrange("(p b) s -> b p s", b=2)
-    gate_rows = tab[1].rearrange("(p b) s -> b p s", b=2)
+
+    def blocks(rows):
+        even, odd = (rows.rearrange("(p b) s -> b p s", b=2)[b] for b in range(2))
+        return odd, even
+
+    value_rows, gate_rows, out_rows = blocks(tab[0]), blocks(tab[1]), blocks(out)
     y_rows = y.rearrange("(p b) n -> p (b n)", b=2)
-    out_rows = out.rearrange("(p b) n -> b p n", b=2)
 
     with tc.tile_pool(name="held", bufs=1) as held:
 
@@ -39,11 +42,11 @@ def tile_lookup_vg_addsilu_out_kernel(tc, tab, y, offs, out):
         nc.sync.dma_start(gates[0][:], gate_rows[0])
         nc.sync.dma_start(offsets[:], offs)
         nc.sync.dma_start(gates[1][:], gate_rows[1])
-        nc.scalar.dma_start(stream[:, : n + Y_CUTS[0]], y_rows[:, : n + Y_CUTS[0]])
+        nc.scalar.dma_start(stream[:, Y_CUTS[-1] :], y_rows[:, Y_CUTS[-1] :])
         nc.scalar.dma_start(values[0][:], value_rows[0])
         nc.sync.dma_start(values[1][:], value_rows[1])
         for lo, hi in pieces(Y_CUTS):
-            nc.sync.dma_start(stream[:, n + lo : n + hi], y_rows[:, n + lo : n + hi])
+            nc.sync.dma_start(stream[:, lo:hi], y_rows[:, lo:hi])
 
         opened = [float_tile(f"opened{b}", n) for b in range(2)]
         for b in range(2):
@@ -53,7 +56,7 @@ def tile_lookup_vg_addsilu_out_kernel(tc, tab, y, offs, out):
 
         def add(b, lo, hi):
             picked = values[b][:].indirect(offsets[:, lo // 16 : hi // 16])
-            nc.vector.tensor_tensor(summed[b][:, lo:hi], picked, stream[:, b * n + lo : b * n + hi], ADD)
+            nc.vector.tensor_tensor(summed[b][:, lo:hi], picked, stream[:, (1 - b) * n + lo : (1 - b) * n + hi], ADD)
 
         def multiply(b, lo, hi, into):
             nc.vector.tensor_tensor(into, summed[b][:, lo:hi], opened[b][:, lo:hi], MULT)
@@ -64,11 +67,11 @@ def tile_lookup_vg_addsilu_out_kernel(tc, tab, y, offs, out):
         for lo, hi in halves:
             multiply(0, lo, hi, product[0][:, lo:hi])
         for lo, hi in pieces(STORE_CUTS):
-            nc.sync.dma_start(out_rows[0, :, lo:hi], product[0][:, lo:hi])
+            nc.sync.dma_start(out_rows[0][:, lo:hi], product[0][:, lo:hi])
 
-        for lo, hi in pieces(SUM_CUTS):
+        for lo, hi in SUMS:
             add(1, lo, hi)
         for k, (lo, hi) in enumerate(pieces(STORE_CUTS)):
-            into = stream[:, n + SUM_CUTS[2] : n + SUM_CUTS[2] + hi] if k == 0 else product[1][:, lo:hi]
+            into = stream[:, slice(*SUMS[2])] if k == 0 else product[1][:, lo:hi]
             multiply(1, lo, hi, into)
-            (nc.sync if k % 2 else nc.scalar).dma_start(out_rows[1, :, lo:hi], into)
+            (nc.sync if k % 2 else nc.scalar).dma_start(out_rows[1][:, lo:hi], into)

@@ -8,9 +8,9 @@ SILU = mybir.ActivationFunctionType.Silu
 
 P = 128
 DMA_BLOCK = 256
-Y_CUTS = (0, 128, 448)
-SUMS = ((448, 512), (0, 128), (128, 256), (256, 448))
-STORE_CUTS = (0, 128, 256, 384, 512)
+CUTS = (0, 128, 320, 448, 512)
+QUARTERS = (0, 128, 256, 384, 512)
+SPARE = 64
 
 
 def pieces(cuts):
@@ -28,6 +28,7 @@ def tile_lookup_vg_addsilu_out_kernel(tc, tab, y, offs, out):
 
     value_rows, gate_rows, out_rows = blocks(tab[0]), blocks(tab[1]), blocks(out)
     y_rows = y.rearrange("(p b) n -> p (b n)", b=2)
+    first, second, third, fourth = pieces(CUTS)
 
     with tc.tile_pool(name="held", bufs=1) as held:
 
@@ -37,41 +38,52 @@ def tile_lookup_vg_addsilu_out_kernel(tc, tab, y, offs, out):
         offsets = held.tile([P, n // 16], U16, name="offsets")
         gates = [float_tile(f"gate{b}", places) for b in range(2)]
         values = [float_tile(f"value{b}", places) for b in range(2)]
-        stream = float_tile("stream", 2 * n)
+        landing = float_tile("landing", SPARE + 2 * n)
+        stream = landing[:, SPARE:]
+        moved = float_tile("moved", first[1])
 
         nc.sync.dma_start(gates[0][:], gate_rows[0])
         nc.sync.dma_start(offsets[:], offs)
         nc.sync.dma_start(gates[1][:], gate_rows[1])
-        nc.scalar.dma_start(stream[:, Y_CUTS[-1] :], y_rows[:, Y_CUTS[-1] :])
+        nc.scalar.dma_start(stream[:, fourth[0] :], y_rows[:, fourth[0] :])
         nc.scalar.dma_start(values[0][:], value_rows[0])
         nc.sync.dma_start(values[1][:], value_rows[1])
-        for lo, hi in pieces(Y_CUTS):
-            nc.sync.dma_start(stream[:, lo:hi], y_rows[:, lo:hi])
+        nc.sync.dma_start(stream[:, third[0] : third[1]], y_rows[:, third[0] : third[1]])
+        nc.sync.dma_start(stream[:, : second[1]], y_rows[:, : second[1]])
 
         opened = [float_tile(f"opened{b}", n) for b in range(2)]
         for b in range(2):
             nc.scalar.activation(opened[b][:], gates[b][:].indirect(offsets[:]), SILU)
         summed = [float_tile(f"summed{b}", n) for b in range(2)]
-        product = [float_tile(f"product{b}", n) for b in range(2)]
+        product = float_tile("product", n)
+        last_product = float_tile("last_product", first[1])
 
-        def add(b, lo, hi):
+        def add(b, lo, hi, addend):
             picked = values[b][:].indirect(offsets[:, lo // 16 : hi // 16])
-            nc.vector.tensor_tensor(summed[b][:, lo:hi], picked, stream[:, (1 - b) * n + lo : (1 - b) * n + hi], ADD)
+            nc.vector.tensor_tensor(summed[b][:, lo:hi], picked, addend, ADD)
 
         def multiply(b, lo, hi, into):
             nc.vector.tensor_tensor(into, summed[b][:, lo:hi], opened[b][:, lo:hi], MULT)
 
         halves = pieces((0, n // 2, n))
         for lo, hi in halves:
-            add(0, lo, hi)
+            add(0, lo, hi, stream[:, n + lo : n + hi])
         for lo, hi in halves:
-            multiply(0, lo, hi, product[0][:, lo:hi])
-        for lo, hi in pieces(STORE_CUTS):
-            nc.sync.dma_start(out_rows[0][:, lo:hi], product[0][:, lo:hi])
+            multiply(0, lo, hi, product[:, lo:hi])
+        for lo, hi in pieces(QUARTERS):
+            nc.sync.dma_start(out_rows[0][:, lo:hi], product[:, lo:hi])
 
-        for lo, hi in SUMS:
-            add(1, lo, hi)
-        for k, (lo, hi) in enumerate(pieces(STORE_CUTS)):
-            into = stream[:, slice(*SUMS[2])] if k == 0 else product[1][:, lo:hi]
+        def finish(lo, hi, into, issuer):
             multiply(1, lo, hi, into)
-            (nc.sync if k % 2 else nc.scalar).dma_start(out_rows[1][:, lo:hi], into)
+            issuer.dma_start(out_rows[1][:, lo:hi], into)
+
+        nc.scalar.copy(moved[:], stream[:, : first[1]])
+        quarters = pieces(QUARTERS)
+        width = QUARTERS[1]
+        for lo, hi in (fourth, third, second):
+            add(1, lo, hi, stream[:, lo:hi])
+        finish(*quarters[3], landing[:, :width], nc.scalar)
+        add(1, *first, moved[:])
+        finish(*quarters[2], landing[:, width : 2 * width], nc.sync)
+        finish(*quarters[1], landing[:, 2 * width : 3 * width], nc.scalar)
+        finish(*quarters[0], last_product[:], nc.sync)

@@ -8,9 +8,8 @@ SILU = mybir.ActivationFunctionType.Silu
 
 P = 128
 DMA_BLOCK = 256
-CUTS = (0, 128, 320, 448, 512)
+CUTS = (0, 256, 448, 512)
 QUARTERS = (0, 128, 256, 384, 512)
-SPARE = 64
 
 
 def pieces(cuts):
@@ -28,7 +27,6 @@ def tile_lookup_vg_addsilu_out_kernel(tc, tab, y, offs, out):
 
     value_rows, gate_rows, out_rows = blocks(tab[0]), blocks(tab[1]), blocks(out)
     y_rows = y.rearrange("(p b) n -> p (b n)", b=2)
-    first, second, third, fourth = pieces(CUTS)
 
     with tc.tile_pool(name="held", bufs=1) as held:
 
@@ -38,52 +36,48 @@ def tile_lookup_vg_addsilu_out_kernel(tc, tab, y, offs, out):
         offsets = held.tile([P, n // 16], U16, name="offsets")
         gates = [float_tile(f"gate{b}", places) for b in range(2)]
         values = [float_tile(f"value{b}", places) for b in range(2)]
-        landing = float_tile("landing", SPARE + 2 * n)
-        stream = landing[:, SPARE:]
-        moved = float_tile("moved", first[1])
+        stream = float_tile("stream", 2 * n)
 
         nc.sync.dma_start(gates[0][:], gate_rows[0])
         nc.sync.dma_start(offsets[:], offs)
         nc.sync.dma_start(gates[1][:], gate_rows[1])
-        nc.scalar.dma_start(stream[:, fourth[0] :], y_rows[:, fourth[0] :])
+        nc.scalar.dma_start(stream[:, CUTS[-2] :], y_rows[:, CUTS[-2] :])
         nc.scalar.dma_start(values[0][:], value_rows[0])
         nc.sync.dma_start(values[1][:], value_rows[1])
-        nc.sync.dma_start(stream[:, third[0] : third[1]], y_rows[:, third[0] : third[1]])
-        nc.sync.dma_start(stream[:, : second[1]], y_rows[:, : second[1]])
+        for lo, hi in reversed(pieces(CUTS)[:-1]):
+            nc.sync.dma_start(stream[:, lo:hi], y_rows[:, lo:hi])
 
         opened = [float_tile(f"opened{b}", n) for b in range(2)]
         for b in range(2):
             nc.scalar.activation(opened[b][:], gates[b][:].indirect(offsets[:]), SILU)
         summed = [float_tile(f"summed{b}", n) for b in range(2)]
-        product = float_tile("product", n)
-        last_product = float_tile("last_product", first[1])
+        product = [float_tile(f"product{b}", n) for b in range(2)]
 
-        def add(b, lo, hi, addend):
+        tail = float_tile("tail", QUARTERS[1])
+
+        def add(b, lo, hi, into):
             picked = values[b][:].indirect(offsets[:, lo // 16 : hi // 16])
-            nc.vector.tensor_tensor(summed[b][:, lo:hi], picked, addend, ADD)
-
-        def multiply(b, lo, hi, into):
-            nc.vector.tensor_tensor(into, summed[b][:, lo:hi], opened[b][:, lo:hi], MULT)
+            nc.vector.tensor_tensor(into, picked, stream[:, (1 - b) * n + lo : (1 - b) * n + hi], ADD)
 
         halves = pieces((0, n // 2, n))
         for lo, hi in halves:
-            add(0, lo, hi, stream[:, n + lo : n + hi])
+            add(0, lo, hi, summed[0][:, lo:hi])
         for lo, hi in halves:
-            multiply(0, lo, hi, product[:, lo:hi])
+            nc.vector.tensor_tensor(product[0][:, lo:hi], summed[0][:, lo:hi], opened[0][:, lo:hi], MULT)
         for lo, hi in pieces(QUARTERS):
-            nc.sync.dma_start(out_rows[0][:, lo:hi], product[:, lo:hi])
+            nc.sync.dma_start(out_rows[0][:, lo:hi], product[0][:, lo:hi])
 
-        def finish(lo, hi, into, issuer):
-            multiply(1, lo, hi, into)
-            issuer.dma_start(out_rows[1][:, lo:hi], into)
-
-        nc.scalar.copy(moved[:], stream[:, : first[1]])
+        first, second, third = pieces(CUTS)
         quarters = pieces(QUARTERS)
-        width = QUARTERS[1]
-        for lo, hi in (fourth, third, second):
-            add(1, lo, hi, stream[:, lo:hi])
-        finish(*quarters[3], landing[:, :width], nc.scalar)
-        add(1, *first, moved[:])
-        finish(*quarters[2], landing[:, width : 2 * width], nc.sync)
-        finish(*quarters[1], landing[:, 2 * width : 3 * width], nc.scalar)
-        finish(*quarters[0], last_product[:], nc.sync)
+        start = quarters[3][0]
+        add(1, *third, tail[:, third[0] - start :])
+        add(1, *second, summed[1][:, slice(*second)])
+        add(1, *first, summed[1][:, slice(*first)])
+        nc.scalar.copy(tail[:, : third[0] - start], summed[1][:, start : third[0]])
+        sources = [summed[1][:, lo:hi] for lo, hi in quarters[:3]] + [tail[:]]
+        targets = [product[1][:, lo:hi] for lo, hi in quarters]
+        targets[2] = summed[1][:, start:]
+        for k in reversed(range(4)):
+            lo, hi = quarters[k]
+            nc.vector.tensor_tensor(targets[k], sources[k], opened[1][:, lo:hi], MULT)
+            (nc.scalar if k % 2 else nc.sync).dma_start(out_rows[1][:, lo:hi], targets[k])

import concourse.mybir as mybir

F32 = mybir.dt.float32
U16 = mybir.dt.uint16
ADD = mybir.AluOpType.add
MULT = mybir.AluOpType.mult
SILU = mybir.ActivationFunctionType.Silu

P = 128
DMA_BLOCK = 256
CUTS = (0, 256, 448, 512)
QUARTERS = (0, 128, 256, 384, 512)


def pieces(cuts):
    return list(zip(cuts, cuts[1:]))


def tile_lookup_vg_addsilu_out_kernel(tc, tab, y, offs, out):
    nc = tc.nc
    places = tab.shape[2]
    n = y.shape[1]

    def blocks(rows):
        even, odd = (rows.rearrange("(p b) s -> b p s", b=2)[b] for b in range(2))
        return odd, even

    value_rows, gate_rows, out_rows = blocks(tab[0]), blocks(tab[1]), blocks(out)
    y_rows = y.rearrange("(p b) n -> p (b n)", b=2)

    with tc.tile_pool(name="held", bufs=1) as held:

        def float_tile(name, columns):
            return held.tile([P, columns], F32, name=name, align_bytes=DMA_BLOCK)

        offsets = held.tile([P, n // 16], U16, name="offsets")
        gates = [float_tile(f"gate{b}", places) for b in range(2)]
        values = [float_tile(f"value{b}", places) for b in range(2)]
        stream = float_tile("stream", 2 * n)

        nc.sync.dma_start(gates[0][:], gate_rows[0])
        nc.sync.dma_start(offsets[:], offs)
        nc.sync.dma_start(gates[1][:], gate_rows[1])
        nc.scalar.dma_start(stream[:, CUTS[-2] :], y_rows[:, CUTS[-2] :])
        nc.scalar.dma_start(values[0][:], value_rows[0])
        nc.sync.dma_start(values[1][:], value_rows[1])
        for lo, hi in reversed(pieces(CUTS)[:-1]):
            nc.sync.dma_start(stream[:, lo:hi], y_rows[:, lo:hi])

        opened = [float_tile(f"opened{b}", n) for b in range(2)]
        for b in range(2):
            nc.scalar.activation(opened[b][:], gates[b][:].indirect(offsets[:]), SILU)
        summed = [float_tile(f"summed{b}", n) for b in range(2)]
        product = [float_tile(f"product{b}", n) for b in range(2)]

        tail = float_tile("tail", QUARTERS[1])

        def add(b, lo, hi, into):
            picked = values[b][:].indirect(offsets[:, lo // 16 : hi // 16])
            nc.vector.tensor_tensor(into, picked, stream[:, (1 - b) * n + lo : (1 - b) * n + hi], ADD)

        halves = pieces((0, n // 2, n))
        for lo, hi in halves:
            add(0, lo, hi, summed[0][:, lo:hi])
        for lo, hi in halves:
            nc.vector.tensor_tensor(product[0][:, lo:hi], summed[0][:, lo:hi], opened[0][:, lo:hi], MULT)
        for lo, hi in pieces(QUARTERS):
            nc.sync.dma_start(out_rows[0][:, lo:hi], product[0][:, lo:hi])

        first, second, third = pieces(CUTS)
        quarters = pieces(QUARTERS)
        start = quarters[3][0]
        add(1, *third, tail[:, third[0] - start :])
        add(1, *second, summed[1][:, slice(*second)])
        add(1, *first, summed[1][:, slice(*first)])
        nc.scalar.copy(tail[:, : third[0] - start], summed[1][:, start : third[0]])
        sources = [summed[1][:, lo:hi] for lo, hi in quarters[:3]] + [tail[:]]
        targets = [product[1][:, lo:hi] for lo, hi in quarters]
        targets[2] = summed[1][:, start:]
        for k in reversed(range(4)):
            lo, hi = quarters[k]
            nc.vector.tensor_tensor(targets[k], sources[k], opened[1][:, lo:hi], MULT)
            (nc.scalar if k % 2 else nc.sync).dma_start(out_rows[1][:, lo:hi], targets[k])
